import numpy as np
import ml_dtypes


def mxq(x, axis, fmt="e4m3"):
    dtype, down = {"e4m3": (ml_dtypes.float8_e4m3fn, 7), "e5m2": (ml_dtypes.float8_e5m2, 14)}[fmt]
    v = np.moveaxis(np.asarray(x, np.float32).astype(ml_dtypes.bfloat16).astype(np.float64), axis, -1)
    blocks = v.reshape(v.shape[:-1] + (-1, 32))
    amax = np.abs(blocks).max(-1, keepdims=True)
    byte = np.maximum(np.where(amax > 0, np.frexp(amax)[1] - 1 + 127, 0) - down, 1)
    scale = np.exp2(byte - 127.0)
    codes = (blocks / scale).astype(np.float32).astype(dtype).astype(np.float64)
    return np.moveaxis((codes * scale).reshape(v.shape), -1, axis)


WIDE = False


def mx_kscale(k):
    if not WIDE:
        return np.ones(k)
    levels = np.array([10, -10, 5, -5, 0])
    if k % 512:
        return np.exp2(np.random.permutation(np.resize(levels, k // 32))).repeat(32)
    a = np.empty((k // 512, 16))
    for p in range(k // 512):
        a[p, :8] = np.random.permutation(np.resize(levels, 8))
        for g in range(8):
            far = levels[np.abs(levels - a[p, g]) >= 10]
            a[p, g + 8] = far[np.random.randint(len(far))]
    return np.exp2(a.ravel()).repeat(32)


def f64(x):
    return np.asarray(x).astype(np.float64)


def striped(idx):
    return np.tile(np.asarray(idx).reshape(-1, 16).T, (8, 1)).astype(np.uint16)


def unstriped(offs):
    return offs[:16].T.reshape(-1).astype(np.int64)


E2M1 = np.array([0.0, 0.5, 1.0, 1.5, 2.0, 3.0, 4.0, 6.0, -0.0, -0.5, -1.0, -1.5, -2.0, -3.0, -4.0, -6.0])


def pack_weight(w, fmt):
    k, n = w.shape
    w = f64(np.asarray(w, np.float32).astype(ml_dtypes.bfloat16)).reshape(k // 32, 32, n)
    amax = np.abs(w).max(1)
    if fmt == "e4m3":
        byte = np.frexp(amax)[1] - 1 + 127 - 7
    else:
        mant, ex = np.frexp(amax / 6.0)
        byte = np.where(mant > 0.5, ex, ex - 1) + 127
    byte = np.clip(np.where(amax > 0, byte, 1), 1, 254)
    scaled = (w * np.exp2(127.0 - byte)[:, None, :]).reshape(k, n).astype(np.float32)
    by_word = np.ascontiguousarray(scaled.reshape(k // 512, 128, 4, n).transpose(0, 1, 3, 2))
    if fmt == "e4m3":
        words = by_word.astype(ml_dtypes.float8_e4m3fn).view(np.uint8)
    else:
        c = by_word.astype(ml_dtypes.float4_e2m1fn).view(np.uint8) & 0xF
        words = (c[..., 0::2] | (c[..., 1::2] << 4)).reshape(k // 512, 128, 2 * n)
    return np.ascontiguousarray(words), np.ascontiguousarray(byte.astype(np.uint8).reshape(k // 512, 16, n))


def unpack_weight(words, scales, fmt):
    g, _, n = scales.shape
    words = np.ascontiguousarray(words).reshape(g, 128, n, -1)
    if fmt == "e4m3":
        vals = words.view(ml_dtypes.float8_e4m3fn).astype(np.float64)
    else:
        nib = np.empty((g, 128, n, 4), np.uint8)
        nib[..., 0::2] = words & 0xF
        nib[..., 1::2] = words >> 4
        vals = E2M1[nib]
    vals = vals * np.repeat(np.exp2(scales.astype(np.float64) - 127.0), 8, axis=1)[..., None]
    return vals.transpose(0, 1, 3, 2).reshape(g * 512, n)


D, T, I, Q, E, Z, M = 512, 2048, 512, 256, 512, 1024, 1024


def setup_inputs():
    n = np.random.standard_normal
    idx = np.random.permutation(T)[:I]
    idx2 = np.random.permutation(Z)[:I]
    idx3 = np.random.permutation(M)[:Q]
    fd = mx_kscale(D)
    fi = mx_kscale(I)
    ti = np.ones(T)
    ti[idx] = fi
    keysp = pack_weight(n((D, T)) / fd[:, None], "e4m3")
    return {
        "query": (n((D, Q)) * 1.0 / np.sqrt(D) * fd[:, None]).astype(np.float32),
        "query2": (n((D, Q)) * 1.0 / np.sqrt(D) * fd[:, None]).astype(np.float32),
        "keys_words": keysp[0],
        "keys_scales": keysp[1],
        "pages": (n((D, Z)) / fd[:, None]).astype(np.float32),
        "os": (np.random.uniform(0.02, 0.08, (1, I)) * fi).astype(np.float32),
        "vals": (n((E, T)) / ti).astype(np.float32),
        "member": (n((E, M))).astype(np.float32),
        "offs": striped(idx),
        "offs2": striped(idx2),
        "offs3": striped(idx3),
    }


def reference(query, query2, keys_words, keys_scales, pages, os, vals, member, offs, offs2, offs3):
    idx = unstriped(offs)
    idx2 = unstriped(offs2)
    idx3 = unstriped(offs3)
    keysu = unpack_weight(keys_words, keys_scales, "e4m3")
    queryq = mxq(f64(query), 0, "e4m3")
    a = queryq.T @ keysu
    query2q = mxq(f64(query2), 0, "e4m3")
    pagesq = mxq(f64(pages), 0, "e4m3")
    h0 = query2q.T @ pagesq
    s = np.maximum(a[:, idx], h0[:, idx2])
    w = np.maximum(s, 0.0)
    wo1 = w * f64(os)
    wt1 = wo1.T
    vt1 = f64(vals)[:, idx].T
    vt1q = mxq(vt1, 0, "e4m3")
    wt1q = mxq(wt1, 0, "e4m3")
    o = vt1q.T @ wt1q
    y = np.abs(o - f64(member)[:, idx3])
    return y

@@ -1,0 +1,242 @@
+from contextlib import ExitStack
+
+import concourse.mybir as mybir
+from concourse.masks import make_identity
+
+D, T, I, Q, E, Z, M = 512, 2048, 512, 256, 512, 1024, 1024
+FLOPS = 2 * Q * D * (T + Z) + 2 * E * I * Q
+
+F32 = mybir.dt.float32
+BF16 = mybir.dt.bfloat16
+I32 = mybir.dt.int32
+U32 = mybir.dt.uint32
+U16 = mybir.dt.uint16
+U8 = mybir.dt.uint8
+FP8X4 = mybir.dt.float8_e4m3fn_x4
+ALU = mybir.AluOpType
+ACT = mybir.ActivationFunctionType
+
+P = 128
+PACK = 4
+BANK = 512
+
+
+def tile_attend_crosslarger_distanceout_lean_kernel(
+    tc, query, query2, keys_words, keys_scales, pages, slot_factor, vals, member, offs, offs2, offs3, out
+):
+    nc = tc.nc
+    with ExitStack() as ctx:
+        sb = ctx.enter_context(tc.tile_pool(name="sb", bufs=1))
+        ps = ctx.enter_context(tc.psum_pool(name="ps", bufs=1))
+
+        def load_rows(name, src):
+            raw = sb.tile([P, PACK, src.shape[1]], F32, name=name)
+            nc.sync.dma_start(out=raw[:], in_=src.rearrange("(p t) c -> p t c", t=PACK))
+            return raw
+
+        def load_list(name, src):
+            lst = sb.tile([P, src.shape[1]], U16, name=name)
+            nc.sync.dma_start(lst[:], src)
+            return lst
+
+        def weave(copy, woven, raw, c0, c1):
+            copy(
+                woven[:, c0:c1, :].rearrange("p (c i) t -> p c t i", i=PACK),
+                raw[:, :, c0:c1].rearrange("p t (c i) -> p c t i", i=PACK),
+            )
+
+        def quantise(name, woven, tag=None):
+            width = woven.shape[1]
+            codes = sb.tile([P, width], U32, name=name + "_codes", tag=tag or name + "_codes", align_bytes=64)
+            scales = sb.tile([P, width], U8, name=name + "_scales", align_bytes=64)
+            nc.vector.quantize_mx(
+                out=codes[:].bitcast(FP8X4), scales=scales[:], in_=woven.rearrange("p c t -> p (c t)")
+            )
+            return codes, scales
+
+        key_planes = sb.tile([P, BANK], U8, name="key_planes", align_bytes=64)
+        scale_words = keys_scales[0].bitcast(I32)
+        for quad in range(4):
+            nc.sync.dma_start(
+                out=key_planes[32 * quad : 32 * quad + 16, :].bitcast(I32),
+                in_=scale_words[4 * quad : 4 * quad + 4, :].rearrange("r (j c) -> j r c", j=4),
+            )
+        ident = sb.tile([P, P], F32, name="ident")
+        make_identity(nc, ident[:])
+
+        q_raw = load_rows("q_raw", query)
+        key_rows = keys_words[0].rearrange("p n t -> p (n t)")
+        key_halves = []
+        for half in range(2):
+            words = sb.tile([P, T // 2], U32, name="keys%d" % half, align_bytes=64)
+            nc.sync.dma_start(
+                out=words[:].bitcast(I32), in_=key_rows[:, half * 2 * T : (half + 1) * 2 * T].bitcast(I32)
+            )
+            key_halves.append(words)
+        q2_raw = load_rows("q2_raw", query2)
+        tok_list = load_list("tok_list", offs)
+        page_raw = [load_rows("page_raw0", pages[:, :BANK])]
+        page_list = load_list("page_list", offs2)
+        page_raw.append(load_rows("page_raw1", pages[:, BANK:]))
+        factor = sb.tile([P, PACK], F32, name="factor")
+        nc.sync.dma_start(out=factor[:], in_=slot_factor.rearrange("o (p t) -> (o p) t", t=PACK))
+        val_rows = []
+        for j in range(4):
+            rows = sb.tile([P, T], F32, name="vals%d" % j, tag="vals%d" % j, align_bytes=64)
+            nc.sync.dma_start(out=rows[:], in_=vals[j * P : (j + 1) * P, :])
+            val_rows.append(rows)
+        member_list = load_list("member_list", offs3)
+        member_rows = []
+        for j in range(4):
+            rows = sb.tile([P, M], F32, name="member%d" % j, tag="member%d" % j, align_bytes=64)
+            nc.sync.dma_start(out=rows[:], in_=member[j * P : (j + 1) * P, :])
+            member_rows.append(rows)
+
+        banks = [ps.tile([P, BANK], F32, name="bank%d" % b) for b in range(8)]
+        woven = sb.tile([P, BANK, PACK], BF16, name="woven", align_bytes=64)
+
+        def weave_and_quantise(name, raw):
+            width = raw.shape[2]
+            weave(nc.vector.tensor_copy, woven, raw, 0, width)
+            return quantise(name, woven[:, :width, :])
+
+        def scores(dst, copy, bank, codes, scales, h, rhs, rhs_scale):
+            nc.tensor.matmul_mx(
+                out=bank[:],
+                lhsT=codes[:, h * P : (h + 1) * P].bitcast(FP8X4),
+                lhsT_scale=scales[:, h * P : (h + 1) * P],
+                rhs=rhs.bitcast(FP8X4),
+                rhs_scale=rhs_scale,
+                start=True,
+                stop=True,
+            )
+            copy(dst, bank[:])
+
+        q_codes, q_scales = weave_and_quantise("q", q_raw)
+        a_rows = [sb.tile([P, T], F32, name="a%d" % h) for h in range(2)]
+        for j in range(4):
+            for h in range(2):
+                scores(
+                    a_rows[h][:, j * BANK : (j + 1) * BANK],
+                    nc.scalar.copy,
+                    banks[2 * j + h],
+                    q_codes, q_scales, h,
+                    key_halves[j // 2][:, (j % 2) * BANK : (j % 2 + 1) * BANK],
+                    key_planes[4 * j : P, :],
+                )
+        a_picked = [sb.tile([P, I], F32, name="a_picked%d" % h) for h in range(2)]
+        for h in range(2):
+            nc.scalar.activation(a_picked[h][:], a_rows[h][:].indirect(tok_list[:]), ACT.Copy)
+
+        q2_codes, q2_scales = weave_and_quantise("q2", q2_raw)
+        h_rows = [sb.tile([P, Z], F32, name="h%d" % h) for h in range(2)]
+        for j in range(2):
+            codes, scales = weave_and_quantise("page%d" % j, page_raw[j])
+            for h in range(2):
+                scores(
+                    h_rows[h][:, j * BANK : (j + 1) * BANK],
+                    nc.vector.tensor_copy if (j, h) == (1, 1) else nc.scalar.copy,
+                    banks[2 * j + h],
+                    q2_codes, q2_scales, h, codes[:], scales[:],
+                )
+        h_picked = [sb.tile([P, I], F32, name="h_picked%d" % h) for h in range(2)]
+        nc.scalar.activation(h_picked[0][:], h_rows[0][:].indirect(page_list[:]), ACT.Copy)
+        nc.vector.tensor_copy(h_picked[1][:], h_rows[1][:].indirect(page_list[:]))
+
+        w_woven = sb.tile([P, Q, PACK], BF16, name="w_woven", align_bytes=64)
+        larger = [sb.tile([P, PACK, P], F32, name="larger%d" % h) for h in range(2)]
+        for h in range(2):
+            nc.vector.tensor_tensor(
+                larger[h][:].rearrange("p t (c i) -> p c t i", i=PACK),
+                a_picked[h][:].rearrange("p (c i t) -> p c t i", i=PACK, t=PACK),
+                h_picked[h][:].rearrange("p (c i t) -> p c t i", i=PACK, t=PACK),
+                ALU.max,
+            )
+            turned = banks[4 + h][:].rearrange("p (t q) -> p t q", t=PACK)
+            for t in range(PACK):
+                nc.tensor.transpose(turned[:, t, :], larger[h][:, t, :], ident[:])
+            nc.vector.scalar_tensor_tensor(
+                w_woven[:, h * P : (h + 1) * P, :],
+                turned.rearrange("p t q -> p q t"),
+                0.0,
+                factor[:].unsqueeze(1).to_broadcast([P, P, PACK]),
+                ALU.max,
+                ALU.mult,
+            )
+        w_codes, w_scales = quantise("w", w_woven[:])
+
+        first_pairs = woven[:].rearrange("p c t -> p (c t)").bitcast(F32)[:, : I // 2]
+        val_pairs = [
+            first_pairs,
+            first_pairs,
+            a_picked[0][:, : I // 2],
+            larger[0][:].rearrange("p t q -> p (t q)")[:, : I // 2],
+        ]
+        def gather_values(j):
+            listed = val_rows[j][:].indirect(tok_list[:])
+            if j == 0:
+                nc.vector.tensor_copy(val_pairs[j].bitcast(BF16), listed)
+            else:
+                nc.scalar.activation(val_pairs[j].bitcast(BF16), listed, ACT.Copy)
+            turned = banks[2 + j][:, : 2 * P].rearrange("p (u e) -> p u e", u=2)
+            for u in range(2):
+                nc.tensor.transpose(turned[:, u, :], val_pairs[j][:, u : I // 2 : 2], ident[:])
+            return turned
+
+        def weave_values(j, turned):
+            val_woven = sb.tile(
+                [P, P, PACK], BF16, name="val_woven%d" % j, tag=("vw0", "vals2", "vals3", "vw3")[j], align_bytes=64
+            )
+            nc.scalar.copy(val_woven[:].bitcast(F32), turned.rearrange("p u e -> p e u"))
+            return val_woven
+
+        def product(j, val_woven):
+            codes, scales = quantise("val%d" % j, val_woven[:], (None, None, "member0", "member1")[j])
+            acc = banks[(3, 6, 7, 0)[j]][:, :Q]
+            nc.tensor.matmul_mx(
+                out=acc,
+                lhsT=codes[:].bitcast(FP8X4),
+                lhsT_scale=scales[:],
+                rhs=w_codes[:].bitcast(FP8X4),
+                rhs_scale=w_scales[:],
+                start=True,
+                stop=True,
+            )
+            return acc
+
+        def finish(j, diff):
+            dist = sb.tile([P, Q], F32, name="dist%d" % j)
+            nc.scalar.activation(dist[:], diff[:], ACT.Abs)
+            nc.sync.dma_start(out=out[j * P : (j + 1) * P, :], in_=dist[:])
+
+        def gather_members(j):
+            cols = sb.tile([P, Q], F32, name="member_picked%d" % j)
+            nc.vector.tensor_copy(cols[:], member_rows[j][:].indirect(member_list[:]))
+            return cols
+
+        def subtract(j, acc, cols):
+            diff = sb.tile([P, Q], F32, name="diff%d" % j)
+            nc.vector.tensor_tensor(diff[:], acc, cols[:], ALU.subtract)
+            finish(j, diff)
+
+        woven0 = weave_values(0, gather_values(0))
+        turned1 = gather_values(1)
+        turned2 = gather_values(2)
+        woven1 = weave_values(1, turned1)
+        turned3 = gather_values(3)
+        woven2 = weave_values(2, turned2)
+        woven3 = weave_values(3, turned3)
+        acc0 = product(0, woven0)
+        acc1 = product(1, woven1)
+        cols0 = gather_members(0)
+        acc2 = product(2, woven2)
+        subtract(0, acc0, cols0)
+        cols1 = gather_members(1)
+        acc3 = product(3, woven3)
+        subtract(1, acc1, cols1)
+        sums = sb.tile([P, Q], F32, name="sums")
+        nc.scalar.copy(sums[:], acc3)
+        subtract(2, acc2, gather_members(2))
+        diff = sb.tile([P, Q], F32, name="diff3")
+        nc.vector.tensor_tensor(diff[:], member_rows[3][:].indirect(member_list[:]), sums[:], ALU.subtract)
+        finish(3, diff)

@@ -54,6 +54,7 @@ def tile_attend_crosslarger_distanceout_lean_kernel(
             )
             return codes, scales
 
+        q_raw = load_rows("q_raw", query)
         key_planes = sb.tile([P, BANK], U8, name="key_planes", align_bytes=64)
         scale_words = keys_scales[0].bitcast(I32)
         for quad in range(4):
@@ -64,7 +65,6 @@ def tile_attend_crosslarger_distanceout_lean_kernel(
         ident = sb.tile([P, P], F32, name="ident")
         make_identity(nc, ident[:])
 
-        q_raw = load_rows("q_raw", query)
         key_rows = keys_words[0].rearrange("p n t -> p (n t)")
         key_halves = []
         for half in range(2):
@@ -86,11 +86,11 @@ def tile_attend_crosslarger_distanceout_lean_kernel(
             nc.sync.dma_start(out=rows[:], in_=vals[j * P : (j + 1) * P, :])
             val_rows.append(rows)
         member_list = load_list("member_list", offs3)
-        member_rows = []
-        for j in range(4):
+        member_rows = {}
+        for j in (1, 2, 3, 0):
             rows = sb.tile([P, M], F32, name="member%d" % j, tag="member%d" % j, align_bytes=64)
             nc.sync.dma_start(out=rows[:], in_=member[j * P : (j + 1) * P, :])
-            member_rows.append(rows)
+            member_rows[j] = rows
 
         banks = [ps.tile([P, BANK], F32, name="bank%d" % b) for b in range(8)]
         woven = sb.tile([P, BANK, PACK], BF16, name="woven", align_bytes=64)
@@ -129,19 +129,19 @@ def tile_attend_crosslarger_distanceout_lean_kernel(
             nc.scalar.activation(a_picked[h][:], a_rows[h][:].indirect(tok_list[:]), ACT.Copy)
 
         q2_codes, q2_scales = weave_and_quantise("q2", q2_raw)
-        h_rows = [sb.tile([P, Z], F32, name="h%d" % h) for h in range(2)]
+        h_rows = [sb.tile([P, Z], F32, name="h%d" % h, tag="h%d" % h, align_bytes=64) for h in range(2)]
         for j in range(2):
             codes, scales = weave_and_quantise("page%d" % j, page_raw[j])
             for h in range(2):
                 scores(
                     h_rows[h][:, j * BANK : (j + 1) * BANK],
-                    nc.vector.tensor_copy if (j, h) == (1, 1) else nc.scalar.copy,
+                    nc.vector.tensor_copy if (j, h) == (1, 0) else nc.scalar.copy,
                     banks[2 * j + h],
                     q2_codes, q2_scales, h, codes[:], scales[:],
                 )
         h_picked = [sb.tile([P, I], F32, name="h_picked%d" % h) for h in range(2)]
-        nc.scalar.activation(h_picked[0][:], h_rows[0][:].indirect(page_list[:]), ACT.Copy)
-        nc.vector.tensor_copy(h_picked[1][:], h_rows[1][:].indirect(page_list[:]))
+        nc.vector.tensor_copy(h_picked[0][:], h_rows[0][:].indirect(page_list[:]))
+        nc.scalar.activation(h_picked[1][:], h_rows[1][:].indirect(page_list[:]), ACT.Copy)
 
         w_woven = sb.tile([P, Q, PACK], BF16, name="w_woven", align_bytes=64)
         larger = [sb.tile([P, PACK, P], F32, name="larger%d" % h) for h in range(2)]
@@ -185,13 +185,13 @@ def tile_attend_crosslarger_distanceout_lean_kernel(
 
         def weave_values(j, turned):
             val_woven = sb.tile(
-                [P, P, PACK], BF16, name="val_woven%d" % j, tag=("vw0", "vals2", "vals3", "vw3")[j], align_bytes=64
+                [P, P, PACK], BF16, name="val_woven%d" % j, tag=("h1", "vals2", "vals3", "vw3")[j], align_bytes=64
             )
             nc.scalar.copy(val_woven[:].bitcast(F32), turned.rearrange("p u e -> p e u"))
             return val_woven
 
         def product(j, val_woven):
-            codes, scales = quantise("val%d" % j, val_woven[:], (None, None, "member0", "member1")[j])
+            codes, scales = quantise("val%d" % j, val_woven[:], (None, None, "member1", "member2")[j])
             acc = banks[(3, 6, 7, 0)[j]][:, :Q]
             nc.tensor.matmul_mx(
                 out=acc,
@@ -205,13 +205,17 @@ def tile_attend_crosslarger_distanceout_lean_kernel(
             return acc
 
         def finish(j, diff):
-            dist = sb.tile([P, Q], F32, name="dist%d" % j)
+            dist = sb.tile([P, Q], F32, name="dist%d" % j, tag=("dist0", "dist1", "member3", "dist3")[j], align_bytes=64)
             nc.scalar.activation(dist[:], diff[:], ACT.Abs)
             nc.sync.dma_start(out=out[j * P : (j + 1) * P, :], in_=dist[:])
 
         def gather_members(j):
             cols = sb.tile([P, Q], F32, name="member_picked%d" % j)
-            nc.vector.tensor_copy(cols[:], member_rows[j][:].indirect(member_list[:]))
+            listed = member_rows[j][:].indirect(member_list[:])
+            if j == 3:
+                nc.scalar.activation(cols[:], listed, ACT.Copy)
+            else:
+                nc.vector.tensor_copy(cols[:], listed)
             return cols
 
         def subtract(j, acc, cols):
@@ -228,15 +232,15 @@ def tile_attend_crosslarger_distanceout_lean_kernel(
         woven3 = weave_values(3, turned3)
         acc0 = product(0, woven0)
         acc1 = product(1, woven1)
-        cols0 = gather_members(0)
-        acc2 = product(2, woven2)
-        subtract(0, acc0, cols0)
+        sums = sb.tile([P, Q], F32, name="sums", tag="vals3", align_bytes=64)
+        nc.scalar.copy(sums[:], acc0)
         cols1 = gather_members(1)
-        acc3 = product(3, woven3)
+        acc2 = product(2, woven2)
         subtract(1, acc1, cols1)
-        sums = sb.tile([P, Q], F32, name="sums")
-        nc.scalar.copy(sums[:], acc3)
-        subtract(2, acc2, gather_members(2))
-        diff = sb.tile([P, Q], F32, name="diff3")
-        nc.vector.tensor_tensor(diff[:], member_rows[3][:].indirect(member_list[:]), sums[:], ALU.subtract)
-        finish(3, diff)
+        cols2 = gather_members(2)
+        acc3 = product(3, woven3)
+        subtract(2, acc2, cols2)
+        subtract(3, acc3, gather_members(3))
+        diff = sb.tile([P, Q], F32, name="diff0")
+        nc.vector.tensor_tensor(diff[:], member_rows[0][:].indirect(member_list[:]), sums[:], ALU.subtract)
+        finish(0, diff)

from contextlib import ExitStack

import concourse.mybir as mybir
from concourse.masks import make_identity

D, T, I, Q, E, Z, M = 512, 2048, 512, 256, 512, 1024, 1024
FLOPS = 2 * Q * D * (T + Z) + 2 * E * I * Q

F32 = mybir.dt.float32
BF16 = mybir.dt.bfloat16
I32 = mybir.dt.int32
U32 = mybir.dt.uint32
U16 = mybir.dt.uint16
U8 = mybir.dt.uint8
FP8X4 = mybir.dt.float8_e4m3fn_x4
ALU = mybir.AluOpType
ACT = mybir.ActivationFunctionType

P = 128
PACK = 4
BANK = 512


def tile_attend_crosslarger_distanceout_lean_kernel(
    tc, query, query2, keys_words, keys_scales, pages, slot_factor, vals, member, offs, offs2, offs3, out
):
    nc = tc.nc
    with ExitStack() as ctx:
        sb = ctx.enter_context(tc.tile_pool(name="sb", bufs=1))
        ps = ctx.enter_context(tc.psum_pool(name="ps", bufs=1))

        def load_rows(name, src):
            raw = sb.tile([P, PACK, src.shape[1]], F32, name=name)
            nc.sync.dma_start(out=raw[:], in_=src.rearrange("(p t) c -> p t c", t=PACK))
            return raw

        def load_list(name, src):
            lst = sb.tile([P, src.shape[1]], U16, name=name)
            nc.sync.dma_start(lst[:], src)
            return lst

        def weave(copy, woven, raw, c0, c1):
            copy(
                woven[:, c0:c1, :].rearrange("p (c i) t -> p c t i", i=PACK),
                raw[:, :, c0:c1].rearrange("p t (c i) -> p c t i", i=PACK),
            )

        def quantise(name, woven, tag=None):
            width = woven.shape[1]
            codes = sb.tile([P, width], U32, name=name + "_codes", tag=tag or name + "_codes", align_bytes=64)
            scales = sb.tile([P, width], U8, name=name + "_scales", align_bytes=64)
            nc.vector.quantize_mx(
                out=codes[:].bitcast(FP8X4), scales=scales[:], in_=woven.rearrange("p c t -> p (c t)")
            )
            return codes, scales

        q_raw = load_rows("q_raw", query)
        key_planes = sb.tile([P, BANK], U8, name="key_planes", align_bytes=64)
        scale_words = keys_scales[0].bitcast(I32)
        for quad in range(4):
            nc.sync.dma_start(
                out=key_planes[32 * quad : 32 * quad + 16, :].bitcast(I32),
                in_=scale_words[4 * quad : 4 * quad + 4, :].rearrange("r (j c) -> j r c", j=4),
            )
        ident = sb.tile([P, P], F32, name="ident")
        make_identity(nc, ident[:])

        key_rows = keys_words[0].rearrange("p n t -> p (n t)")
        key_halves = []
        for half in range(2):
            words = sb.tile([P, T // 2], U32, name="keys%d" % half, align_bytes=64)
            nc.sync.dma_start(
                out=words[:].bitcast(I32), in_=key_rows[:, half * 2 * T : (half + 1) * 2 * T].bitcast(I32)
            )
            key_halves.append(words)
        q2_raw = load_rows("q2_raw", query2)
        tok_list = load_list("tok_list", offs)
        page_raw = [load_rows("page_raw0", pages[:, :BANK])]
        page_list = load_list("page_list", offs2)
        page_raw.append(load_rows("page_raw1", pages[:, BANK:]))
        factor = sb.tile([P, PACK], F32, name="factor")
        nc.sync.dma_start(out=factor[:], in_=slot_factor.rearrange("o (p t) -> (o p) t", t=PACK))
        val_rows = []
        for j in range(4):
            rows = sb.tile([P, T], F32, name="vals%d" % j, tag="vals%d" % j, align_bytes=64)
            nc.sync.dma_start(out=rows[:], in_=vals[j * P : (j + 1) * P, :])
            val_rows.append(rows)
        member_list = load_list("member_list", offs3)
        member_rows = {}
        for j in (1, 2, 3, 0):
            rows = sb.tile([P, M], F32, name="member%d" % j, tag="member%d" % j, align_bytes=64)
            nc.sync.dma_start(out=rows[:], in_=member[j * P : (j + 1) * P, :])
            member_rows[j] = rows

        banks = [ps.tile([P, BANK], F32, name="bank%d" % b) for b in range(8)]
        woven = sb.tile([P, BANK, PACK], BF16, name="woven", align_bytes=64)

        def weave_and_quantise(name, raw):
            width = raw.shape[2]
            weave(nc.vector.tensor_copy, woven, raw, 0, width)
            return quantise(name, woven[:, :width, :])

        def scores(dst, copy, bank, codes, scales, h, rhs, rhs_scale):
            nc.tensor.matmul_mx(
                out=bank[:],
                lhsT=codes[:, h * P : (h + 1) * P].bitcast(FP8X4),
                lhsT_scale=scales[:, h * P : (h + 1) * P],
                rhs=rhs.bitcast(FP8X4),
                rhs_scale=rhs_scale,
                start=True,
                stop=True,
            )
            copy(dst, bank[:])

        q_codes, q_scales = weave_and_quantise("q", q_raw)
        a_rows = [sb.tile([P, T], F32, name="a%d" % h) for h in range(2)]
        for j in range(4):
            for h in range(2):
                scores(
                    a_rows[h][:, j * BANK : (j + 1) * BANK],
                    nc.scalar.copy,
                    banks[2 * j + h],
                    q_codes, q_scales, h,
                    key_halves[j // 2][:, (j % 2) * BANK : (j % 2 + 1) * BANK],
                    key_planes[4 * j : P, :],
                )
        a_picked = [sb.tile([P, I], F32, name="a_picked%d" % h) for h in range(2)]
        for h in range(2):
            nc.scalar.activation(a_picked[h][:], a_rows[h][:].indirect(tok_list[:]), ACT.Copy)

        q2_codes, q2_scales = weave_and_quantise("q2", q2_raw)
        h_rows = [sb.tile([P, Z], F32, name="h%d" % h, tag="h%d" % h, align_bytes=64) for h in range(2)]
        for j in range(2):
            codes, scales = weave_and_quantise("page%d" % j, page_raw[j])
            for h in range(2):
                scores(
                    h_rows[h][:, j * BANK : (j + 1) * BANK],
                    nc.vector.tensor_copy if (j, h) == (1, 0) else nc.scalar.copy,
                    banks[2 * j + h],
                    q2_codes, q2_scales, h, codes[:], scales[:],
                )
        h_picked = [sb.tile([P, I], F32, name="h_picked%d" % h) for h in range(2)]
        nc.vector.tensor_copy(h_picked[0][:], h_rows[0][:].indirect(page_list[:]))
        nc.scalar.activation(h_picked[1][:], h_rows[1][:].indirect(page_list[:]), ACT.Copy)

        w_woven = sb.tile([P, Q, PACK], BF16, name="w_woven", align_bytes=64)
        larger = [sb.tile([P, PACK, P], F32, name="larger%d" % h) for h in range(2)]
        for h in range(2):
            nc.vector.tensor_tensor(
                larger[h][:].rearrange("p t (c i) -> p c t i", i=PACK),
                a_picked[h][:].rearrange("p (c i t) -> p c t i", i=PACK, t=PACK),
                h_picked[h][:].rearrange("p (c i t) -> p c t i", i=PACK, t=PACK),
                ALU.max,
            )
            turned = banks[4 + h][:].rearrange("p (t q) -> p t q", t=PACK)
            for t in range(PACK):
                nc.tensor.transpose(turned[:, t, :], larger[h][:, t, :], ident[:])
            nc.vector.scalar_tensor_tensor(
                w_woven[:, h * P : (h + 1) * P, :],
                turned.rearrange("p t q -> p q t"),
                0.0,
                factor[:].unsqueeze(1).to_broadcast([P, P, PACK]),
                ALU.max,
                ALU.mult,
            )
        w_codes, w_scales = quantise("w", w_woven[:])

        first_pairs = woven[:].rearrange("p c t -> p (c t)").bitcast(F32)[:, : I // 2]
        val_pairs = [
            first_pairs,
            first_pairs,
            a_picked[0][:, : I // 2],
            larger[0][:].rearrange("p t q -> p (t q)")[:, : I // 2],
        ]
        def gather_values(j):
            listed = val_rows[j][:].indirect(tok_list[:])
            if j == 0:
                nc.vector.tensor_copy(val_pairs[j].bitcast(BF16), listed)
            else:
                nc.scalar.activation(val_pairs[j].bitcast(BF16), listed, ACT.Copy)
            turned = banks[2 + j][:, : 2 * P].rearrange("p (u e) -> p u e", u=2)
            for u in range(2):
                nc.tensor.transpose(turned[:, u, :], val_pairs[j][:, u : I // 2 : 2], ident[:])
            return turned

        def weave_values(j, turned):
            val_woven = sb.tile(
                [P, P, PACK], BF16, name="val_woven%d" % j, tag=("h1", "vals2", "vals3", "vw3")[j], align_bytes=64
            )
            nc.scalar.copy(val_woven[:].bitcast(F32), turned.rearrange("p u e -> p e u"))
            return val_woven

        def product(j, val_woven):
            codes, scales = quantise("val%d" % j, val_woven[:], (None, None, "member1", "member2")[j])
            acc = banks[(3, 6, 7, 0)[j]][:, :Q]
            nc.tensor.matmul_mx(
                out=acc,
                lhsT=codes[:].bitcast(FP8X4),
                lhsT_scale=scales[:],
                rhs=w_codes[:].bitcast(FP8X4),
                rhs_scale=w_scales[:],
                start=True,
                stop=True,
            )
            return acc

        def finish(j, diff):
            dist = sb.tile([P, Q], F32, name="dist%d" % j, tag=("dist0", "dist1", "member3", "dist3")[j], align_bytes=64)
            nc.scalar.activation(dist[:], diff[:], ACT.Abs)
            nc.sync.dma_start(out=out[j * P : (j + 1) * P, :], in_=dist[:])

        def gather_members(j):
            cols = sb.tile([P, Q], F32, name="member_picked%d" % j)
            listed = member_rows[j][:].indirect(member_list[:])
            if j == 3:
                nc.scalar.activation(cols[:], listed, ACT.Copy)
            else:
                nc.vector.tensor_copy(cols[:], listed)
            return cols

        def subtract(j, acc, cols):
            diff = sb.tile([P, Q], F32, name="diff%d" % j)
            nc.vector.tensor_tensor(diff[:], acc, cols[:], ALU.subtract)
            finish(j, diff)

        woven0 = weave_values(0, gather_values(0))
        turned1 = gather_values(1)
        turned2 = gather_values(2)
        woven1 = weave_values(1, turned1)
        turned3 = gather_values(3)
        woven2 = weave_values(2, turned2)
        woven3 = weave_values(3, turned3)
        acc0 = product(0, woven0)
        acc1 = product(1, woven1)
        sums = sb.tile([P, Q], F32, name="sums", tag="vals3", align_bytes=64)
        nc.scalar.copy(sums[:], acc0)
        cols1 = gather_members(1)
        acc2 = product(2, woven2)
        subtract(1, acc1, cols1)
        cols2 = gather_members(2)
        acc3 = product(3, woven3)
        subtract(2, acc2, cols2)
        subtract(3, acc3, gather_members(3))
        diff = sb.tile([P, Q], F32, name="diff0")
        nc.vector.tensor_tensor(diff[:], member_rows[0][:].indirect(member_list[:]), sums[:], ALU.subtract)
        finish(0, diff)
